import numpy as np
import ml_dtypes


def mxq(x, axis, fmt="e4m3"):
    dtype, down = {"e4m3": (ml_dtypes.float8_e4m3fn, 7), "e5m2": (ml_dtypes.float8_e5m2, 14)}[fmt]
    v = np.moveaxis(np.asarray(x, np.float32).astype(ml_dtypes.bfloat16).astype(np.float64), axis, -1)
    blocks = v.reshape(v.shape[:-1] + (-1, 32))
    amax = np.abs(blocks).max(-1, keepdims=True)
    byte = np.maximum(np.where(amax > 0, np.frexp(amax)[1] - 1 + 127, 0) - down, 1)
    scale = np.exp2(byte - 127.0)
    codes = (blocks / scale).astype(np.float32).astype(dtype).astype(np.float64)
    return np.moveaxis((codes * scale).reshape(v.shape), -1, axis)


WIDE = False


def mx_kscale(k, group=512):
    if not WIDE:
        return np.ones(k)
    levels = np.array([18, -18])
    if group != 512:
        return np.exp2(np.random.permutation(np.resize(levels, k // group))).repeat(group)
    if k % 512:
        return np.exp2(np.random.permutation(np.resize(levels, k // 32))).repeat(32)
    a = np.empty((k // 512, 16))
    for p in range(k // 512):
        a[p, :8] = np.random.permutation(np.resize(levels, 8))
        for g in range(8):
            far = levels[np.abs(levels - a[p, g]) >= 10]
            a[p, g + 8] = far[np.random.randint(len(far))]
    return np.exp2(a.ravel()).repeat(32)


def f64(x):
    return np.asarray(x).astype(np.float64)


def bf(x):
    return np.asarray(x, np.float32).astype(ml_dtypes.bfloat16)


def planes(Y):
    r, m = Y.shape
    b = f64(bf(Y)).reshape(r // 32, 32, m)
    amax = np.abs(b).max(1)
    byte = np.clip(np.where(amax > 0, np.frexp(amax)[1] - 1 + 127 - 7, 1), 1, 254)
    codes = (b * np.exp2(127.0 - byte)[:, None, :]).reshape(r, m).astype(np.float32).astype(ml_dtypes.float8_e4m3fn).view(np.uint8)
    words = codes.reshape(r // 512, 128, 4, m).transpose(0, 1, 3, 2)
    return np.ascontiguousarray(words), np.ascontiguousarray(byte.astype(np.uint8).reshape(r // 512, 16, m))


G, D, M, N = 4, 128, 128, 512


def setup_inputs():
    n = np.random.standard_normal
    s_d = mx_kscale(D, 0)
    return {
        "xr": (n((G, D, N)) * s_d[:, None]).astype(np.float32),
        "xi": (n((G, D, N)) * s_d[:, None]).astype(np.float32),
        "wr": (n((G, D, M)) / np.sqrt(D) / s_d[:, None]).astype(np.float32),
        "wi": (n((G, D, M)) / np.sqrt(D) / s_d[:, None]).astype(np.float32),
    }


def reference(xr, xi, wr, wi):
    wrq = mxq(f64(wr), 1, "e4m3")
    xrq = mxq(f64(xr), 1, "e4m3")
    rr = wrq.transpose(0, 2, 1) @ xrq
    wiq = mxq(f64(wi), 1, "e4m3")
    xiq = mxq(f64(xi), 1, "e4m3")
    ii = wiq.transpose(0, 2, 1) @ xiq
    yi = (wrq.transpose(0, 2, 1) @ xiq) + (wiq.transpose(0, 2, 1) @ xrq)
    yr = rr - ii
    y = np.sqrt(np.square(yr) + np.square(yi) + 0.0001)
    Y = y.reshape(G * M, N)
    words, scales = planes(Y)
    return Y, words, scales

@@ -1,0 +1,200 @@
+from contextlib import ExitStack
+
+import concourse.mybir as mybir
+
+G, D, M, N = 4, 128, 128, 512
+FLOPS = 4 * 2 * G * D * M * N
+
+F32 = mybir.dt.float32
+BF16 = mybir.dt.bfloat16
+I32 = mybir.dt.int32
+U32 = mybir.dt.uint32
+U8 = mybir.dt.uint8
+FP8X4 = mybir.dt.float8_e4m3fn_x4
+ACT = mybir.ActivationFunctionType
+ALU = mybir.AluOpType
+
+P = 128
+PACK = 4
+ROWS = 32
+W = 128
+CHUNKS = N // W
+EPS = 1e-4
+
+
+def tile_rows_pl_cplx_mag_kernel(tc, xr, xi, wr, wi, out_0, out_1, out_2):
+    nc = tc.nc
+
+    def by_feature(t):
+        return t.rearrange("g (p j) n -> (g p) j n", j=PACK)
+
+    def read_order(raw):
+        return raw.rearrange("p j (c i) -> p c j i", i=4)
+
+    def write_order(packed):
+        return packed.rearrange("p (c i) j -> p c j i", i=4)
+
+    def quantize(codes, scales, packed):
+        nc.vector.quantize_mx(out=codes.bitcast(FP8X4), scales=scales, in_=packed.rearrange("p n j -> p (n j)"))
+
+    y_hbm = out_0.rearrange("(g m) n -> m g n", g=G)
+    words_hbm = out_1[0].rearrange("p n u -> p (n u)").bitcast(I32)
+    scales_hbm = out_2[0].bitcast(I32)
+
+    with ExitStack() as ctx:
+        sb = ctx.enter_context(tc.tile_pool(name="sb", bufs=1))
+        ps = ctx.enter_context(tc.psum_pool(name="ps", bufs=1))
+        ctx.enter_context(tc.manual_schedule())
+
+        def tile(name, shape, dtype):
+            return sb.tile(shape, dtype, name=name, align_bytes=64)
+
+        wr_raw = tile("wr_raw", [P, PACK, M], F32)
+        wi_raw = tile("wi_raw", [P, PACK, M], F32)
+        w_pos = tile("w_pos", [P, 2 * M, PACK], BF16)
+        w_neg = tile("w_neg", [P, M, PACK], BF16)
+        wp_codes = tile("wp_codes", [P, 2 * M], U32)
+        wp_scales = tile("wp_scales", [P, 2 * M], U8)
+        wn_codes = tile("wn_codes", [P, M], U32)
+        wn_scales = tile("wn_scales", [P, M], U8)
+        one = tile("one", [P, 1], F32)
+        eps = tile("eps", [P, 1], F32)
+
+        x_raw, x_packed, x_codes, x_scales = {}, {}, {}, {}
+        for c in range(CHUNKS):
+            for part in "ri":
+                x_raw[part, c] = tile("x%s_raw%d" % (part, c), [P, PACK, W], F32)
+                x_packed[part, c] = tile("x%s_packed%d" % (part, c), [P, W, PACK], BF16)
+                x_codes[part, c] = tile("x%s_codes%d" % (part, c), [P, W], U32)
+                x_scales[part, c] = tile("x%s_scales%d" % (part, c), [P, W], U8)
+        banks = {}
+        for g in range(G):
+            for b in range(2):
+                banks[g, b] = ps.tile([P, 512], F32, name="bank%d_%d" % (g, b))
+        squares = {(c, h): tile("squares%d_%d" % (c, h), [P, 2, 2, W], F32) for c in range(CHUNKS) for h in range(2)}
+        sums = {(c, h): tile("sums%d_%d" % (c, h), [P, 2, W], F32) for c in range(CHUNKS) for h in range(2)}
+        spans = [(0, 2), (2, 3), (3, 4)]
+        span_of = {c: s for s, (a, b) in enumerate(spans) for c in range(a, b)}
+        y = [tile("y%d" % s, [P, G, (b - a) * W], F32) for s, (a, b) in enumerate(spans)]
+        y_rows = [tile("y_rows%d" % s, [P, PACK, (b - a) * W], F32) for s, (a, b) in enumerate(spans)]
+        y_packed = [tile("y_packed%d" % s, [P, (b - a) * W, PACK], BF16) for s, (a, b) in enumerate(spans)]
+        y_codes = tile("y_codes", [P, N], U32)
+        y_scales = tile("y_scales", [P, N], U8)
+
+        def load_x(c):
+            for part, src in (("r", xr), ("i", xi)):
+                nc.sync.dma_start(out=x_raw[part, c][:], in_=by_feature(src)[:, :, c * W : (c + 1) * W])
+
+        def pack_x(part, c, on_scalar=False):
+            dst, src = write_order(x_packed[part, c][:]), read_order(x_raw[part, c][:])
+            if on_scalar:
+                nc.scalar.copy(out=dst, in_=src)
+            else:
+                nc.vector.tensor_copy(out=dst, in_=src)
+
+        def quantize_x(part, c):
+            quantize(x_codes[part, c][:], x_scales[part, c][:], x_packed[part, c][:])
+
+        def products(c):
+            w_r = (wp_codes, wp_scales, slice(0, M))
+            w_i = (wp_codes, wp_scales, slice(M, 2 * M))
+            w_n = (wn_codes, wn_scales, slice(0, M))
+            passes = [(w_r, "r", 0, True), (w_n, "i", 0, False), (w_i, "r", 1, True), (w_r, "i", 1, False)]
+            for (codes, scales, cols), part, region, first in passes:
+                for g in range(G):
+                    rows = slice(ROWS * g, ROWS * (g + 1))
+                    nc.tensor.matmul_mx(
+                        out=banks[g, c % 2][:, region * W : (region + 1) * W],
+                        lhsT=codes[rows, cols].bitcast(FP8X4),
+                        lhsT_scale=scales[rows, cols],
+                        rhs=x_codes[part, c][rows, :].bitcast(FP8X4),
+                        rhs_scale=x_scales[part, c][rows, :],
+                        start=first,
+                        stop=not first,
+                    )
+
+        def square(c, g):
+            nc.scalar.activation(
+                out=squares[c, g // 2][:, g % 2, :, :].rearrange("p r n -> p (r n)"),
+                in_=banks[g, c % 2][:, 0 : 2 * W],
+                func=ACT.Square,
+            )
+
+        def add(c, h):
+            nc.vector.tensor_tensor(out=sums[c, h][:], in0=squares[c, h][:, :, 0, :], in1=squares[c, h][:, :, 1, :], op=ALU.add)
+
+        def root(c, h):
+            s = span_of[c]
+            o = (c - spans[s][0]) * W
+            nc.scalar.activation(out=y[s][:, 2 * h : 2 * h + 2, o : o + W], in_=sums[c, h][:], func=ACT.Sqrt, bias=eps[:])
+
+        def regroup(s, g):
+            nc.sync.dma_start(out=y_rows[s][ROWS * g : ROWS * (g + 1), :, :], in_=y[s][:, g, :])
+
+        def store_y(s):
+            a, b = spans[s]
+            nc.sync.dma_start(out=y_hbm[:, :, a * W : b * W], in_=y[s][:])
+
+        def pack_y(s):
+            nc.vector.tensor_copy(out=write_order(y_packed[s][:]), in_=read_order(y_rows[s][:]))
+
+        def quantize_y(s):
+            a, b = spans[s]
+            quantize(y_codes[:, a * W : b * W], y_scales[:, a * W : b * W], y_packed[s][:])
+
+        def store_words(a, b):
+            nc.sync.dma_start(out=words_hbm[:, a * W : b * W], in_=y_codes[:, a * W : b * W].bitcast(I32))
+
+        nc.sync.dma_start(out=wr_raw[:], in_=by_feature(wr))
+        nc.sync.dma_start(out=wi_raw[:], in_=by_feature(wi))
+        for c in range(CHUNKS):
+            load_x(c)
+
+        nc.vector.memset(one[:], 1.0)
+        nc.scalar.activation(out=eps[:], in_=one[:], func=ACT.Sqrt, scale=EPS * EPS)
+
+        nc.vector.tensor_copy(out=write_order(w_pos[:, 0:M, :]), in_=read_order(wr_raw[:]))
+        nc.vector.tensor_copy(out=write_order(w_pos[:, M : 2 * M, :]), in_=read_order(wi_raw[:]))
+        nc.scalar.activation(out=write_order(w_neg[:]), in_=read_order(wi_raw[:]), func=ACT.Copy, scale=-1.0)
+        pack_x("r", 0, on_scalar=True)
+        quantize(wp_codes[:], wp_scales[:], w_pos[:])
+        quantize(wn_codes[:], wn_scales[:], w_neg[:])
+        pack_x("i", 0)
+        quantize_x("r", 0)
+        quantize_x("i", 0)
+        products(0)
+        pack_x("r", 1, on_scalar=True)
+
+        for c in range(CHUNKS):
+            if c + 1 < CHUNKS:
+                pack_x("i", c + 1)
+                quantize_x("r", c + 1)
+                quantize_x("i", c + 1)
+                products(c + 1)
+            for g in range(G):
+                square(c, g)
+                if g % 2 == 1:
+                    add(c, g // 2)
+            if c + 2 < CHUNKS:
+                pack_x("r", c + 2)
+            s = span_of[c]
+            last = c == spans[s][1] - 1
+            for h in range(2):
+                root(c, h)
+                if last:
+                    regroup(s, 2 * h)
+                    regroup(s, 2 * h + 1)
+            if last:
+                store_y(s)
+
+        pack_y(0)
+        pack_y(1)
+        quantize_y(0)
+        quantize_y(1)
+        store_words(0, 3)
+        pack_y(2)
+        quantize_y(2)
+        store_words(3, 4)
+        for q in range(4):
+            eng = nc.sync if q % 2 == 0 else nc.scalar
+            eng.dma_start(out=scales_hbm[4 * q : 4 * q + 4, :], in_=y_scales[ROWS * q : ROWS * q + 4, :].bitcast(I32))

@@ -17,9 +17,11 @@ ALU = mybir.AluOpType
 P = 128
 PACK = 4
 ROWS = 32
-W = 128
-CHUNKS = N // W
+HALF = N // 2
 EPS = 1e-4
+XI0_ON_VECTOR = 128
+PIECES = [(0, slice(0, 256)), (1, slice(0, 128)), (1, slice(128, 256))]
+PAIRS = [(0, 2), (1, 3)]
 
 
 def tile_rows_pl_cplx_mag_kernel(tc, xr, xi, wr, wi, out_0, out_1, out_2):
@@ -37,7 +39,7 @@ def tile_rows_pl_cplx_mag_kernel(tc, xr, xi, wr, wi, out_0, out_1, out_2):
     def quantize(codes, scales, packed):
         nc.vector.quantize_mx(out=codes.bitcast(FP8X4), scales=scales, in_=packed.rearrange("p n j -> p (n j)"))
 
-    y_hbm = out_0.rearrange("(g m) n -> m g n", g=G)
+    y_hbm = out_0.rearrange("(p u) n -> p u n", u=PACK)
     words_hbm = out_1[0].rearrange("p n u -> p (n u)").bitcast(I32)
     scales_hbm = out_2[0].bitcast(I32)
 
@@ -51,150 +53,127 @@ def tile_rows_pl_cplx_mag_kernel(tc, xr, xi, wr, wi, out_0, out_1, out_2):
 
         wr_raw = tile("wr_raw", [P, PACK, M], F32)
         wi_raw = tile("wi_raw", [P, PACK, M], F32)
-        w_pos = tile("w_pos", [P, 2 * M, PACK], BF16)
-        w_neg = tile("w_neg", [P, M, PACK], BF16)
-        wp_codes = tile("wp_codes", [P, 2 * M], U32)
-        wp_scales = tile("wp_scales", [P, 2 * M], U8)
-        wn_codes = tile("wn_codes", [P, M], U32)
-        wn_scales = tile("wn_scales", [P, M], U8)
+        w_packed = tile("w_packed", [P, 2 * M, PACK], BF16)
+        w_codes = tile("w_codes", [P, 2 * M], U32)
+        w_scales = tile("w_scales", [P, 2 * M], U8)
         one = tile("one", [P, 1], F32)
         eps = tile("eps", [P, 1], F32)
 
-        x_raw, x_packed, x_codes, x_scales = {}, {}, {}, {}
-        for c in range(CHUNKS):
-            for part in "ri":
-                x_raw[part, c] = tile("x%s_raw%d" % (part, c), [P, PACK, W], F32)
-                x_packed[part, c] = tile("x%s_packed%d" % (part, c), [P, W, PACK], BF16)
-                x_codes[part, c] = tile("x%s_codes%d" % (part, c), [P, W], U32)
-                x_scales[part, c] = tile("x%s_scales%d" % (part, c), [P, W], U8)
-        banks = {}
-        for g in range(G):
-            for b in range(2):
-                banks[g, b] = ps.tile([P, 512], F32, name="bank%d_%d" % (g, b))
-        squares = {(c, h): tile("squares%d_%d" % (c, h), [P, 2, 2, W], F32) for c in range(CHUNKS) for h in range(2)}
-        sums = {(c, h): tile("sums%d_%d" % (c, h), [P, 2, W], F32) for c in range(CHUNKS) for h in range(2)}
-        spans = [(0, 2), (2, 3), (3, 4)]
-        span_of = {c: s for s, (a, b) in enumerate(spans) for c in range(a, b)}
-        y = [tile("y%d" % s, [P, G, (b - a) * W], F32) for s, (a, b) in enumerate(spans)]
-        y_rows = [tile("y_rows%d" % s, [P, PACK, (b - a) * W], F32) for s, (a, b) in enumerate(spans)]
-        y_packed = [tile("y_packed%d" % s, [P, (b - a) * W, PACK], BF16) for s, (a, b) in enumerate(spans)]
+        def halves(name, shape, dtype):
+            return [tile("%s%d" % (name, h), shape, dtype) for h in range(2)]
+
+        xr_raw = halves("xr_raw", [P, PACK, HALF], F32)
+        xi_raw = halves("xi_raw", [P, PACK, HALF], F32)
+        xr_packed = halves("xr_packed", [P, HALF, PACK], BF16)
+        xn_packed = halves("xn_packed", [P, HALF, PACK], BF16)
+        xi_packed = halves("xi_packed", [P, HALF, PACK], BF16)
+        x_codes = halves("x_codes", [P, 3 * HALF], U32)
+        x_scales = halves("x_scales", [P, 3 * HALF], U8)
+
+        banks = [[ps.tile([P, 2, HALF], F32, name="bank%d_%d" % (h, g)) for g in range(G)] for h in range(2)]
+        widths = [c.stop - c.start for h, c in PIECES]
+        columns = [slice(h * HALF + c.start, h * HALF + c.stop) for h, c in PIECES]
+        squares = [tile("squares%d" % k, [P, G, 2, w], F32) for k, w in enumerate(widths)]
+        sums = [tile("sums%d" % k, [P, G, w], F32) for k, w in enumerate(widths)]
+        sums_rows = [tile("sums_rows%d" % k, [P, PACK, w], F32) for k, w in enumerate(widths)]
+        y = [tile("y%d" % k, [P, PACK, w], F32) for k, w in enumerate(widths)]
+        y_packed = [tile("y_packed%d" % k, [P, w, PACK], BF16) for k, w in enumerate(widths)]
         y_codes = tile("y_codes", [P, N], U32)
         y_scales = tile("y_scales", [P, N], U8)
 
-        def load_x(c):
-            for part, src in (("r", xr), ("i", xi)):
-                nc.sync.dma_start(out=x_raw[part, c][:], in_=by_feature(src)[:, :, c * W : (c + 1) * W])
+        def pack(packed, raw):
+            nc.vector.tensor_copy(out=write_order(packed), in_=read_order(raw))
 
-        def pack_x(part, c, on_scalar=False):
-            dst, src = write_order(x_packed[part, c][:]), read_order(x_raw[part, c][:])
-            if on_scalar:
-                nc.scalar.copy(out=dst, in_=src)
-            else:
-                nc.vector.tensor_copy(out=dst, in_=src)
+        def negate_xr(h):
+            nc.scalar.activation(out=write_order(xn_packed[h][:]), in_=read_order(xr_raw[h][:]), func=ACT.Copy, scale=-1.0)
 
-        def quantize_x(part, c):
-            quantize(x_codes[part, c][:], x_scales[part, c][:], x_packed[part, c][:])
+        def quantize_x(h, place, packed):
+            cols = slice(place * HALF, (place + 1) * HALF)
+            quantize(x_codes[h][:, cols], x_scales[h][:, cols], packed[h][:])
 
-        def products(c):
-            w_r = (wp_codes, wp_scales, slice(0, M))
-            w_i = (wp_codes, wp_scales, slice(M, 2 * M))
-            w_n = (wn_codes, wn_scales, slice(0, M))
-            passes = [(w_r, "r", 0, True), (w_n, "i", 0, False), (w_i, "r", 1, True), (w_r, "i", 1, False)]
-            for (codes, scales, cols), part, region, first in passes:
-                for g in range(G):
+        def products(h):
+            for step in range(2):
+                w_cols = slice(step * M, (step + 1) * M)
+                x_cols = slice(step * HALF, (step + 2) * HALF)
+                for g in (0, 2, 1, 3):
                     rows = slice(ROWS * g, ROWS * (g + 1))
                     nc.tensor.matmul_mx(
-                        out=banks[g, c % 2][:, region * W : (region + 1) * W],
-                        lhsT=codes[rows, cols].bitcast(FP8X4),
-                        lhsT_scale=scales[rows, cols],
-                        rhs=x_codes[part, c][rows, :].bitcast(FP8X4),
-                        rhs_scale=x_scales[part, c][rows, :],
-                        start=first,
-                        stop=not first,
+                        out=banks[h][g][:].rearrange("p r n -> p (r n)"),
+                        lhsT=w_codes[rows, w_cols].bitcast(FP8X4),
+                        lhsT_scale=w_scales[rows, w_cols],
+                        rhs=x_codes[h][rows, x_cols].bitcast(FP8X4),
+                        rhs_scale=x_scales[h][rows, x_cols],
+                        start=step == 0,
+                        stop=step == 1,
                     )
 
-        def square(c, g):
-            nc.scalar.activation(
-                out=squares[c, g // 2][:, g % 2, :, :].rearrange("p r n -> p (r n)"),
-                in_=banks[g, c % 2][:, 0 : 2 * W],
-                func=ACT.Square,
-            )
+        def square(k, g):
+            h, cols = PIECES[k]
+            nc.scalar.activation(out=squares[k][:, g, :, :], in_=banks[h][g][:, :, cols], func=ACT.Square)
 
-        def add(c, h):
-            nc.vector.tensor_tensor(out=sums[c, h][:], in0=squares[c, h][:, :, 0, :], in1=squares[c, h][:, :, 1, :], op=ALU.add)
+        def add(k, pair):
+            groups = slice(pair[0], G, 2)
+            nc.vector.tensor_tensor(out=sums[k][:, groups, :], in0=squares[k][:, groups, 0, :], in1=squares[k][:, groups, 1, :], op=ALU.add)
 
-        def root(c, h):
-            s = span_of[c]
-            o = (c - spans[s][0]) * W
-            nc.scalar.activation(out=y[s][:, 2 * h : 2 * h + 2, o : o + W], in_=sums[c, h][:], func=ACT.Sqrt, bias=eps[:])
-
-        def regroup(s, g):
-            nc.sync.dma_start(out=y_rows[s][ROWS * g : ROWS * (g + 1), :, :], in_=y[s][:, g, :])
-
-        def store_y(s):
-            a, b = spans[s]
-            nc.sync.dma_start(out=y_hbm[:, :, a * W : b * W], in_=y[s][:])
-
-        def pack_y(s):
-            nc.vector.tensor_copy(out=write_order(y_packed[s][:]), in_=read_order(y_rows[s][:]))
-
-        def quantize_y(s):
-            a, b = spans[s]
-            quantize(y_codes[:, a * W : b * W], y_scales[:, a * W : b * W], y_packed[s][:])
-
-        def store_words(a, b):
-            nc.sync.dma_start(out=words_hbm[:, a * W : b * W], in_=y_codes[:, a * W : b * W].bitcast(I32))
+        def regroup(k, g, eng):
+            eng.dma_start(out=sums_rows[k][ROWS * g : ROWS * (g + 1), :, :], in_=sums[k][:, g, :])
 
         nc.sync.dma_start(out=wr_raw[:], in_=by_feature(wr))
         nc.sync.dma_start(out=wi_raw[:], in_=by_feature(wi))
-        for c in range(CHUNKS):
-            load_x(c)
+        for h in range(2):
+            cols = slice(h * HALF, (h + 1) * HALF)
+            nc.sync.dma_start(out=xr_raw[h][:], in_=by_feature(xr)[:, :, cols])
+            nc.sync.dma_start(out=xi_raw[h][:], in_=by_feature(xi)[:, :, cols])
 
         nc.vector.memset(one[:], 1.0)
         nc.scalar.activation(out=eps[:], in_=one[:], func=ACT.Sqrt, scale=EPS * EPS)
 
-        nc.vector.tensor_copy(out=write_order(w_pos[:, 0:M, :]), in_=read_order(wr_raw[:]))
-        nc.vector.tensor_copy(out=write_order(w_pos[:, M : 2 * M, :]), in_=read_order(wi_raw[:]))
-        nc.scalar.activation(out=write_order(w_neg[:]), in_=read_order(wi_raw[:]), func=ACT.Copy, scale=-1.0)
-        pack_x("r", 0, on_scalar=True)
-        quantize(wp_codes[:], wp_scales[:], w_pos[:])
-        quantize(wn_codes[:], wn_scales[:], w_neg[:])
-        pack_x("i", 0)
-        quantize_x("r", 0)
-        quantize_x("i", 0)
+        pack(w_packed[:, 0:M, :], wr_raw[:])
+        pack(w_packed[:, M : 2 * M, :], wi_raw[:])
+        negate_xr(0)
+        pack(xr_packed[0][:], xr_raw[0][:])
+        quantize(w_codes[:], w_scales[:], w_packed[:])
+        quantize_x(0, 2, xr_packed)
+        nc.scalar.copy(out=write_order(xi_packed[0][:, XI0_ON_VECTOR:, :]), in_=read_order(xi_raw[0][:, :, XI0_ON_VECTOR:]))
+        pack(xi_packed[0][:, :XI0_ON_VECTOR, :], xi_raw[0][:, :, :XI0_ON_VECTOR])
+        quantize_x(0, 0, xn_packed)
+        quantize_x(0, 1, xi_packed)
         products(0)
-        pack_x("r", 1, on_scalar=True)
 
-        for c in range(CHUNKS):
-            if c + 1 < CHUNKS:
-                pack_x("i", c + 1)
-                quantize_x("r", c + 1)
-                quantize_x("i", c + 1)
-                products(c + 1)
-            for g in range(G):
-                square(c, g)
-                if g % 2 == 1:
-                    add(c, g // 2)
-            if c + 2 < CHUNKS:
-                pack_x("r", c + 2)
-            s = span_of[c]
-            last = c == spans[s][1] - 1
-            for h in range(2):
-                root(c, h)
-                if last:
-                    regroup(s, 2 * h)
-                    regroup(s, 2 * h + 1)
-            if last:
-                store_y(s)
+        negate_xr(1)
+        pack(xr_packed[1][:], xr_raw[1][:])
+        quantize_x(1, 2, xr_packed)
+        pack(xi_packed[1][:], xi_raw[1][:])
+        quantize_x(1, 0, xn_packed)
+        quantize_x(1, 1, xi_packed)
+        products(1)
 
-        pack_y(0)
-        pack_y(1)
-        quantize_y(0)
-        quantize_y(1)
-        store_words(0, 3)
-        pack_y(2)
-        quantize_y(2)
-        store_words(3, 4)
+        last = len(PIECES) - 1
+        waiting = []
+        for k in range(len(PIECES)):
+            for pair in PAIRS:
+                square(k, pair[0])
+                square(k, pair[1])
+                for args in waiting:
+                    regroup(*args, nc.scalar)
+                waiting.clear()
+                add(k, pair)
+                regroup(k, pair[0], nc.sync)
+                if k == 0:
+                    regroup(k, pair[1], nc.gpsimd)
+                else:
+                    waiting.append((k, pair[1]))
+        regroup(*waiting[0], nc.scalar)
+
+        for k, cols in enumerate(columns):
+            nc.scalar.activation(out=y[k][:], in_=sums_rows[k][:], func=ACT.Sqrt, bias=eps[:])
+            eng = nc.scalar if k == last else nc.sync
+            eng.dma_start(out=y_hbm[:, :, cols], in_=y[k][:])
+            pack(y_packed[k][:], y[k][:])
+            quantize(y_codes[:, cols], y_scales[:, cols], y_packed[k][:])
+            if k > 0:
+                done = slice(0 if k == 1 else cols.start, cols.stop)
+                nc.sync.dma_start(out=words_hbm[:, done], in_=y_codes[:, done].bitcast(I32))
         for q in range(4):
             eng = nc.sync if q % 2 == 0 else nc.scalar
             eng.dma_start(out=scales_hbm[4 * q : 4 * q + 4, :], in_=y_scales[ROWS * q : ROWS * q + 4, :].bitcast(I32))

@@ -17,11 +17,13 @@ ALU = mybir.AluOpType
 P = 128
 PACK = 4
 ROWS = 32
-HALF = N // 2
+W = 128
+CHUNKS = N // W
+WINDOW = 4
+SLOTS = 3 * CHUNKS + 3
 EPS = 1e-4
-XI0_ON_VECTOR = 128
-PIECES = [(0, slice(0, 256)), (1, slice(0, 128)), (1, slice(128, 256))]
 PAIRS = [(0, 2), (1, 3)]
+SPANS = [(0, 1), (1, 3), (3, 4)]
 
 
 def tile_rows_pl_cplx_mag_kernel(tc, xr, xi, wr, wi, out_0, out_1, out_2):
@@ -39,6 +41,9 @@ def tile_rows_pl_cplx_mag_kernel(tc, xr, xi, wr, wi, out_0, out_1, out_2):
     def quantize(codes, scales, packed):
         nc.vector.quantize_mx(out=codes.bitcast(FP8X4), scales=scales, in_=packed.rearrange("p n j -> p (n j)"))
 
+    def columns(first, last):
+        return slice(first * W, last * W)
+
     y_hbm = out_0.rearrange("(p u) n -> p u n", u=PACK)
     words_hbm = out_1[0].rearrange("p n u -> p (n u)").bitcast(I32)
     scales_hbm = out_2[0].bitcast(I32)
@@ -51,129 +56,173 @@ def tile_rows_pl_cplx_mag_kernel(tc, xr, xi, wr, wi, out_0, out_1, out_2):
         def tile(name, shape, dtype):
             return sb.tile(shape, dtype, name=name, align_bytes=64)
 
+        def per_chunk(name, shape, dtype):
+            return [tile("%s%d" % (name, c), shape, dtype) for c in range(CHUNKS)]
+
         wr_raw = tile("wr_raw", [P, PACK, M], F32)
         wi_raw = tile("wi_raw", [P, PACK, M], F32)
-        w_packed = tile("w_packed", [P, 2 * M, PACK], BF16)
-        w_codes = tile("w_codes", [P, 2 * M], U32)
-        w_scales = tile("w_scales", [P, 2 * M], U8)
+        w_pos = tile("w_pos", [P, 2 * M, PACK], BF16)
+        w_neg = tile("w_neg", [P, M, PACK], BF16)
+        w_codes = tile("w_codes", [P, 3 * M], U32)
+        w_scales = tile("w_scales", [P, 3 * M], U8)
         one = tile("one", [P, 1], F32)
         eps = tile("eps", [P, 1], F32)
 
-        def halves(name, shape, dtype):
-            return [tile("%s%d" % (name, h), shape, dtype) for h in range(2)]
+        xr_raw = per_chunk("xr_raw", [P, PACK, W], F32)
+        xi_raw = per_chunk("xi_raw", [P, PACK, W], F32)
+        xr_packed = per_chunk("xr_packed", [P, W, PACK], BF16)
+        xi_packed = per_chunk("xi_packed", [P, W, PACK], BF16)
+        x_codes = tile("x_codes", [P, SLOTS * W], U32)
+        x_scales = tile("x_scales", [P, SLOTS * W], U8)
 
-        xr_raw = halves("xr_raw", [P, PACK, HALF], F32)
-        xi_raw = halves("xi_raw", [P, PACK, HALF], F32)
-        xr_packed = halves("xr_packed", [P, HALF, PACK], BF16)
-        xn_packed = halves("xn_packed", [P, HALF, PACK], BF16)
-        xi_packed = halves("xi_packed", [P, HALF, PACK], BF16)
-        x_codes = halves("x_codes", [P, 3 * HALF], U32)
-        x_scales = halves("x_scales", [P, 3 * HALF], U8)
-
-        banks = [[ps.tile([P, 2, HALF], F32, name="bank%d_%d" % (h, g)) for g in range(G)] for h in range(2)]
-        widths = [c.stop - c.start for h, c in PIECES]
-        columns = [slice(h * HALF + c.start, h * HALF + c.stop) for h, c in PIECES]
-        squares = [tile("squares%d" % k, [P, G, 2, w], F32) for k, w in enumerate(widths)]
-        sums = [tile("sums%d" % k, [P, G, w], F32) for k, w in enumerate(widths)]
-        sums_rows = [tile("sums_rows%d" % k, [P, PACK, w], F32) for k, w in enumerate(widths)]
-        y = [tile("y%d" % k, [P, PACK, w], F32) for k, w in enumerate(widths)]
-        y_packed = [tile("y_packed%d" % k, [P, w, PACK], BF16) for k, w in enumerate(widths)]
+        banks = [[ps.tile([P, WINDOW * W], F32, name="bank%d_%d" % (b, g)) for g in range(G)] for b in range(2)]
+        squares = per_chunk("squares", [P, G, 2, W], F32)
+        span_of = {c: s for s, (a, b) in enumerate(SPANS) for c in range(a, b)}
+        sums = [tile("sums%d" % s, [P, G, (b - a) * W], F32) for s, (a, b) in enumerate(SPANS)]
+        sums_rows = [tile("sums_rows%d" % s, [P, PACK, (b - a) * W], F32) for s, (a, b) in enumerate(SPANS)]
+        y = [tile("y%d" % s, [P, PACK, (b - a) * W], F32) for s, (a, b) in enumerate(SPANS)]
+        y_packed = per_chunk("y_packed", [P, W, PACK], BF16)
         y_codes = tile("y_codes", [P, N], U32)
         y_scales = tile("y_scales", [P, N], U8)
+
+        def within(c):
+            first = c - SPANS[span_of[c]][0]
+            return columns(first, first + 1)
 
         def pack(packed, raw):
             nc.vector.tensor_copy(out=write_order(packed), in_=read_order(raw))
 
-        def negate_xr(h):
-            nc.scalar.activation(out=write_order(xn_packed[h][:]), in_=read_order(xr_raw[h][:]), func=ACT.Copy, scale=-1.0)
+        def pack_on_scalar(packed, raw):
+            nc.scalar.copy(out=write_order(packed), in_=read_order(raw))
 
-        def quantize_x(h, place, packed):
-            cols = slice(place * HALF, (place + 1) * HALF)
-            quantize(x_codes[h][:, cols], x_scales[h][:, cols], packed[h][:])
+        def product(c, step):
+            w_cols = slice((1, 0, 2)[step] * M, ((1, 0, 2)[step] + 1) * M)
+            x_cols = columns(3 * c + step, 3 * c + step + WINDOW)
+            for g in (0, 2, 1, 3):
+                rows = slice(ROWS * g, ROWS * (g + 1))
+                nc.tensor.matmul_mx(
+                    out=banks[c % 2][g][:],
+                    lhsT=w_codes[rows, w_cols].bitcast(FP8X4),
+                    lhsT_scale=w_scales[rows, w_cols],
+                    rhs=x_codes[rows, x_cols].bitcast(FP8X4),
+                    rhs_scale=x_scales[rows, x_cols],
+                    start=step == 0,
+                    stop=step == 2,
+                )
 
-        def products(h):
-            for step in range(2):
-                w_cols = slice(step * M, (step + 1) * M)
-                x_cols = slice(step * HALF, (step + 2) * HALF)
-                for g in (0, 2, 1, 3):
-                    rows = slice(ROWS * g, ROWS * (g + 1))
-                    nc.tensor.matmul_mx(
-                        out=banks[h][g][:].rearrange("p r n -> p (r n)"),
-                        lhsT=w_codes[rows, w_cols].bitcast(FP8X4),
-                        lhsT_scale=w_scales[rows, w_cols],
-                        rhs=x_codes[h][rows, x_cols].bitcast(FP8X4),
-                        rhs_scale=x_scales[h][rows, x_cols],
-                        start=step == 0,
-                        stop=step == 1,
-                    )
+        def quantize_xr(c):
+            cols = columns(3 * c + 3, 3 * c + 4)
+            quantize(x_codes[:, cols], x_scales[:, cols], xr_packed[c][:])
+            product(c, 0)
 
-        def square(k, g):
-            h, cols = PIECES[k]
-            nc.scalar.activation(out=squares[k][:, g, :, :], in_=banks[h][g][:, :, cols], func=ACT.Square)
+        def quantize_xi(c):
+            cols = columns(3 * c + 4, 3 * c + 5)
+            quantize(x_codes[:, cols], x_scales[:, cols], xi_packed[c][:])
+            product(c, 1)
+            product(c, 2)
 
-        def add(k, pair):
+        def regroup(s, g, eng):
+            eng.dma_start(out=sums_rows[s][ROWS * g : ROWS * (g + 1), :, :], in_=sums[s][:, g, :])
+
+        def square(c, pair):
+            for g in pair:
+                nc.scalar.activation(
+                    out=squares[c][:, g, :, :].rearrange("p r n -> p (r n)"),
+                    in_=banks[c % 2][g][:, columns(2, 4)],
+                    func=ACT.Square,
+                )
+
+        def add(c, pair):
             groups = slice(pair[0], G, 2)
-            nc.vector.tensor_tensor(out=sums[k][:, groups, :], in0=squares[k][:, groups, 0, :], in1=squares[k][:, groups, 1, :], op=ALU.add)
-
-        def regroup(k, g, eng):
-            eng.dma_start(out=sums_rows[k][ROWS * g : ROWS * (g + 1), :, :], in_=sums[k][:, g, :])
+            nc.vector.tensor_tensor(
+                out=sums[span_of[c]][:, groups, within(c)],
+                in0=squares[c][:, groups, 0, :],
+                in1=squares[c][:, groups, 1, :],
+                op=ALU.add,
+            )
 
         nc.sync.dma_start(out=wr_raw[:], in_=by_feature(wr))
         nc.sync.dma_start(out=wi_raw[:], in_=by_feature(wi))
-        for h in range(2):
-            cols = slice(h * HALF, (h + 1) * HALF)
-            nc.sync.dma_start(out=xr_raw[h][:], in_=by_feature(xr)[:, :, cols])
-            nc.sync.dma_start(out=xi_raw[h][:], in_=by_feature(xi)[:, :, cols])
+        for c in range(CHUNKS):
+            nc.sync.dma_start(out=xr_raw[c][:], in_=by_feature(xr)[:, :, columns(c, c + 1)])
+            nc.sync.dma_start(out=xi_raw[c][:], in_=by_feature(xi)[:, :, columns(c, c + 1)])
 
         nc.vector.memset(one[:], 1.0)
         nc.scalar.activation(out=eps[:], in_=one[:], func=ACT.Sqrt, scale=EPS * EPS)
+        nc.vector.memset(x_codes[:], 0)
+        nc.vector.memset(x_scales[:].bitcast(U32), 0)
 
-        pack(w_packed[:, 0:M, :], wr_raw[:])
-        pack(w_packed[:, M : 2 * M, :], wi_raw[:])
-        negate_xr(0)
-        pack(xr_packed[0][:], xr_raw[0][:])
-        quantize(w_codes[:], w_scales[:], w_packed[:])
-        quantize_x(0, 2, xr_packed)
-        nc.scalar.copy(out=write_order(xi_packed[0][:, XI0_ON_VECTOR:, :]), in_=read_order(xi_raw[0][:, :, XI0_ON_VECTOR:]))
-        pack(xi_packed[0][:, :XI0_ON_VECTOR, :], xi_raw[0][:, :, :XI0_ON_VECTOR])
-        quantize_x(0, 0, xn_packed)
-        quantize_x(0, 1, xi_packed)
-        products(0)
-
-        negate_xr(1)
-        pack(xr_packed[1][:], xr_raw[1][:])
-        quantize_x(1, 2, xr_packed)
+        pack(w_pos[:, 0:M, :], wr_raw[:])
+        pack(w_pos[:, M : 2 * M, :], wi_raw[:])
+        nc.scalar.activation(out=write_order(w_neg[:]), in_=read_order(wi_raw[:]), func=ACT.Copy, scale=-1.0)
+        pack_on_scalar(xr_packed[0][:], xr_raw[0][:])
+        pack_on_scalar(xr_packed[1][:], xr_raw[1][:])
+        quantize(w_codes[:, 0 : 2 * M], w_scales[:, 0 : 2 * M], w_pos[:])
+        quantize(w_codes[:, 2 * M : 3 * M], w_scales[:, 2 * M : 3 * M], w_neg[:])
+        quantize_xr(0)
+        pack(xi_packed[0][:], xi_raw[0][:])
+        quantize_xi(0)
         pack(xi_packed[1][:], xi_raw[1][:])
-        quantize_x(1, 0, xn_packed)
-        quantize_x(1, 1, xi_packed)
-        products(1)
+        quantize_xr(1)
+        quantize_xi(1)
+        for pair in PAIRS:
+            square(0, pair)
 
-        last = len(PIECES) - 1
+        pack(xr_packed[2][:], xr_raw[2][:])
+        pack(xi_packed[2][:], xi_raw[2][:])
+        quantize_xr(2)
+        quantize_xi(2)
+        for pair in PAIRS:
+            square(1, pair)
+
+        pack(xr_packed[3][:], xr_raw[3][:])
+        add(0, PAIRS[0])
+        quantize_xr(3)
+        pack(xi_packed[3][:], xi_raw[3][:])
+        add(0, PAIRS[1])
+        quantize_xi(3)
+        for g in (0, 2, 1, 3):
+            regroup(0, g, nc.sync)
+        for pair in PAIRS:
+            add(1, pair)
+
         waiting = []
-        for k in range(len(PIECES)):
+        for c in (2, 3):
             for pair in PAIRS:
-                square(k, pair[0])
-                square(k, pair[1])
+                square(c, pair)
                 for args in waiting:
                     regroup(*args, nc.scalar)
                 waiting.clear()
-                add(k, pair)
-                regroup(k, pair[0], nc.sync)
-                if k == 0:
-                    regroup(k, pair[1], nc.gpsimd)
-                else:
-                    waiting.append((k, pair[1]))
+                add(c, pair)
+                regroup(span_of[c], pair[0], nc.sync)
+                waiting.append((span_of[c], pair[1]))
         regroup(*waiting[0], nc.scalar)
 
-        for k, cols in enumerate(columns):
-            nc.scalar.activation(out=y[k][:], in_=sums_rows[k][:], func=ACT.Sqrt, bias=eps[:])
-            eng = nc.scalar if k == last else nc.sync
-            eng.dma_start(out=y_hbm[:, :, cols], in_=y[k][:])
-            pack(y_packed[k][:], y[k][:])
-            quantize(y_codes[:, cols], y_scales[:, cols], y_packed[k][:])
-            if k > 0:
-                done = slice(0 if k == 1 else cols.start, cols.stop)
-                nc.sync.dma_start(out=words_hbm[:, done], in_=y_codes[:, done].bitcast(I32))
+        def root(out, in_):
+            nc.scalar.activation(out=out, in_=in_, func=ACT.Sqrt, bias=eps[:])
+
+        def quantize_y(c):
+            cols = columns(c, c + 1)
+            quantize(y_codes[:, cols], y_scales[:, cols], y_packed[c][:])
+
+        last = CHUNKS - 1
+        for c in range(last):
+            s = span_of[c]
+            root(y[s][:, :, within(c)], sums_rows[s][:, :, within(c)])
+            pack(y_packed[c][:], y[s][:, :, within(c)])
+            if c == SPANS[s][1] - 1:
+                nc.sync.dma_start(out=y_hbm[:, :, columns(*SPANS[s])], in_=y[s][:])
+            if c > 0:
+                quantize_y(c - 1)
+        quantize_y(last - 1)
+        nc.sync.dma_start(out=words_hbm[:, columns(0, last)], in_=y_codes[:, columns(0, last)].bitcast(I32))
+
+        s = span_of[last]
+        root(write_order(y_packed[last][:]), read_order(sums_rows[s][:]))
+        quantize_y(last)
+        root(y[s][:], sums_rows[s][:])
+        nc.sync.dma_start(out=words_hbm[:, columns(last, CHUNKS)], in_=y_codes[:, columns(last, CHUNKS)].bitcast(I32))
+        nc.scalar.dma_start(out=y_hbm[:, :, columns(last, CHUNKS)], in_=y[s][:])
         for q in range(4):
-            eng = nc.sync if q % 2 == 0 else nc.scalar
+            eng = nc.scalar if q == 3 else nc.sync
             eng.dma_start(out=scales_hbm[4 * q : 4 * q + 4, :], in_=y_scales[ROWS * q : ROWS * q + 4, :].bitcast(I32))

@@ -68,7 +68,9 @@ def tile_rows_pl_cplx_mag_kernel(tc, xr, xi, wr, wi, out_0, out_1, out_2):
         one = tile("one", [P, 1], F32)
         eps = tile("eps", [P, 1], F32)
 
-        xr_raw = per_chunk("xr_raw", [P, PACK, W], F32)
+        xr_raw = [tile("xr_raw%d" % h, [P, PACK, 2 * W], F32) for h in range(2)]
+        evicted = tile("evicted", [P, 2 * W], F32)
+        y_last = tile("y_last", [P, G, W], F32)
         xi_raw = per_chunk("xi_raw", [P, PACK, W], F32)
         xr_packed = per_chunk("xr_packed", [P, W, PACK], BF16)
         xi_packed = per_chunk("xi_packed", [P, W, PACK], BF16)
@@ -80,7 +82,7 @@ def tile_rows_pl_cplx_mag_kernel(tc, xr, xi, wr, wi, out_0, out_1, out_2):
         span_of = {c: s for s, (a, b) in enumerate(SPANS) for c in range(a, b)}
         sums = [tile("sums%d" % s, [P, G, (b - a) * W], F32) for s, (a, b) in enumerate(SPANS)]
         sums_rows = [tile("sums_rows%d" % s, [P, PACK, (b - a) * W], F32) for s, (a, b) in enumerate(SPANS)]
-        y = [tile("y%d" % s, [P, PACK, (b - a) * W], F32) for s, (a, b) in enumerate(SPANS)]
+        y = [tile("y%d" % s, [P, PACK, (b - a) * W], F32) for s, (a, b) in enumerate(SPANS[:-1])]
         y_packed = per_chunk("y_packed", [P, W, PACK], BF16)
         y_codes = tile("y_codes", [P, N], U32)
         y_scales = tile("y_scales", [P, N], U8)
@@ -113,7 +115,6 @@ def tile_rows_pl_cplx_mag_kernel(tc, xr, xi, wr, wi, out_0, out_1, out_2):
         def quantize_xr(c):
             cols = columns(3 * c + 3, 3 * c + 4)
             quantize(x_codes[:, cols], x_scales[:, cols], xr_packed[c][:])
-            product(c, 0)
 
         def quantize_xi(c):
             cols = columns(3 * c + 4, 3 * c + 5)
@@ -124,8 +125,8 @@ def tile_rows_pl_cplx_mag_kernel(tc, xr, xi, wr, wi, out_0, out_1, out_2):
         def regroup(s, g, eng):
             eng.dma_start(out=sums_rows[s][ROWS * g : ROWS * (g + 1), :, :], in_=sums[s][:, g, :])
 
-        def square(c, pair):
-            for g in pair:
+        def square(c, groups):
+            for g in groups:
                 nc.scalar.activation(
                     out=squares[c][:, g, :, :].rearrange("p r n -> p (r n)"),
                     in_=banks[c % 2][g][:, columns(2, 4)],
@@ -133,7 +134,7 @@ def tile_rows_pl_cplx_mag_kernel(tc, xr, xi, wr, wi, out_0, out_1, out_2):
                 )
 
         def add(c, pair):
-            groups = slice(pair[0], G, 2)
+            groups = slice(pair[0], pair[-1] + 1, 2)
             nc.vector.tensor_tensor(
                 out=sums[span_of[c]][:, groups, within(c)],
                 in0=squares[c][:, groups, 0, :],
@@ -144,7 +145,8 @@ def tile_rows_pl_cplx_mag_kernel(tc, xr, xi, wr, wi, out_0, out_1, out_2):
         nc.sync.dma_start(out=wr_raw[:], in_=by_feature(wr))
         nc.sync.dma_start(out=wi_raw[:], in_=by_feature(wi))
         for c in range(CHUNKS):
-            nc.sync.dma_start(out=xr_raw[c][:], in_=by_feature(xr)[:, :, columns(c, c + 1)])
+            if c % 2 == 0:
+                nc.sync.dma_start(out=xr_raw[c // 2][:], in_=by_feature(xr)[:, :, columns(c, c + 2)])
             nc.sync.dma_start(out=xi_raw[c][:], in_=by_feature(xi)[:, :, columns(c, c + 1)])
 
         nc.vector.memset(one[:], 1.0)
@@ -155,48 +157,60 @@ def tile_rows_pl_cplx_mag_kernel(tc, xr, xi, wr, wi, out_0, out_1, out_2):
         pack(w_pos[:, 0:M, :], wr_raw[:])
         pack(w_pos[:, M : 2 * M, :], wi_raw[:])
         nc.scalar.activation(out=write_order(w_neg[:]), in_=read_order(wi_raw[:]), func=ACT.Copy, scale=-1.0)
-        pack_on_scalar(xr_packed[0][:], xr_raw[0][:])
-        pack_on_scalar(xr_packed[1][:], xr_raw[1][:])
         quantize(w_codes[:, 0 : 2 * M], w_scales[:, 0 : 2 * M], w_pos[:])
         quantize(w_codes[:, 2 * M : 3 * M], w_scales[:, 2 * M : 3 * M], w_neg[:])
+        pack(xr_packed[0][:], xr_raw[0][:, :, columns(0, 1)])
+        pack_on_scalar(xr_packed[1][:], xr_raw[0][:, :, columns(1, 2)])
         quantize_xr(0)
+        last = CHUNKS - 1
+        product(0, 0)
         pack(xi_packed[0][:], xi_raw[0][:])
-        quantize_xi(0)
-        pack(xi_packed[1][:], xi_raw[1][:])
         quantize_xr(1)
+        quantize_xi(0)
+        square(0, (0, 2, 1, 3))
+        product(1, 0)
+        pack(xi_packed[1][:], xi_raw[1][:])
         quantize_xi(1)
-        for pair in PAIRS:
-            square(0, pair)
-
-        pack(xr_packed[2][:], xr_raw[2][:])
-        pack(xi_packed[2][:], xi_raw[2][:])
+        square(1, (0, 2, 1, 3))
+        pack(xr_packed[2][:], xr_raw[1][:, :, columns(0, 1)])
+        pack(xr_packed[3][:], xr_raw[1][:, :, columns(1, 2)])
         quantize_xr(2)
-        quantize_xi(2)
-        for pair in PAIRS:
-            square(1, pair)
-
-        pack(xr_packed[3][:], xr_raw[3][:])
-        add(0, PAIRS[0])
+        product(2, 0)
+        pack(xi_packed[2][:], xi_raw[2][:])
         quantize_xr(3)
-        pack(xi_packed[3][:], xi_raw[3][:])
+        quantize_xi(2)
+        product(last, 0)
+        add(0, PAIRS[0])
+        pack(xi_packed[last][:], xi_raw[last][:])
         add(0, PAIRS[1])
-        quantize_xi(3)
+        quantize_xi(last)
         for g in (0, 2, 1, 3):
             regroup(0, g, nc.sync)
         for pair in PAIRS:
             add(1, pair)
 
-        waiting = []
-        for c in (2, 3):
-            for pair in PAIRS:
-                square(c, pair)
-                for args in waiting:
-                    regroup(*args, nc.scalar)
-                waiting.clear()
-                add(c, pair)
-                regroup(span_of[c], pair[0], nc.sync)
-                waiting.append((span_of[c], pair[1]))
-        regroup(*waiting[0], nc.scalar)
+        square(2, PAIRS[0])
+        add(2, PAIRS[0])
+        regroup(1, 0, nc.sync)
+        square(2, PAIRS[1])
+        regroup(1, 2, nc.scalar)
+        add(2, PAIRS[1])
+        regroup(1, 1, nc.sync)
+        sums_of_3 = banks[last % 2][3][:, columns(2, 4)]
+        nc.vector.tensor_copy(out=evicted[:], in_=sums_of_3)
+        nc.vector.tensor_tensor(
+            out=squares[last][:, 3, :, :].rearrange("p r n -> p (r n)"), in0=sums_of_3, in1=evicted[:], op=ALU.mult
+        )
+        add(last, (3,))
+        regroup(2, 3, nc.sync)
+        square(last, PAIRS[0])
+        regroup(1, 3, nc.scalar)
+        add(last, PAIRS[0])
+        regroup(2, 0, nc.sync)
+        square(last, (1,))
+        regroup(2, 2, nc.scalar)
+        add(last, (1,))
+        regroup(2, 1, nc.sync)
 
         def root(out, in_):
             nc.scalar.activation(out=out, in_=in_, func=ACT.Sqrt, bias=eps[:])
@@ -205,24 +219,23 @@ def tile_rows_pl_cplx_mag_kernel(tc, xr, xi, wr, wi, out_0, out_1, out_2):
             cols = columns(c, c + 1)
             quantize(y_codes[:, cols], y_scales[:, cols], y_packed[c][:])
 
-        last = CHUNKS - 1
         for c in range(last):
             s = span_of[c]
             root(y[s][:, :, within(c)], sums_rows[s][:, :, within(c)])
             pack(y_packed[c][:], y[s][:, :, within(c)])
             if c == SPANS[s][1] - 1:
                 nc.sync.dma_start(out=y_hbm[:, :, columns(*SPANS[s])], in_=y[s][:])
+            if c == 0:
+                root(y_last[:], sums[2][:])
+                nc.sync.dma_start(out=out_0.rearrange("(g m) n -> m g n", g=G)[:, :, columns(last, CHUNKS)], in_=y_last[:])
             if c > 0:
                 quantize_y(c - 1)
         quantize_y(last - 1)
         nc.sync.dma_start(out=words_hbm[:, columns(0, last)], in_=y_codes[:, columns(0, last)].bitcast(I32))
 
-        s = span_of[last]
-        root(write_order(y_packed[last][:]), read_order(sums_rows[s][:]))
+        root(write_order(y_packed[last][:]), read_order(sums_rows[2][:]))
         quantize_y(last)
-        root(y[s][:], sums_rows[s][:])
         nc.sync.dma_start(out=words_hbm[:, columns(last, CHUNKS)], in_=y_codes[:, columns(last, CHUNKS)].bitcast(I32))
-        nc.scalar.dma_start(out=y_hbm[:, :, columns(last, CHUNKS)], in_=y[s][:])
         for q in range(4):
-            eng = nc.scalar if q == 3 else nc.sync
+            eng = nc.scalar if q % 2 == 0 else nc.sync
             eng.dma_start(out=scales_hbm[4 * q : 4 * q + 4, :], in_=y_scales[ROWS * q : ROWS * q + 4, :].bitcast(I32))

from contextlib import ExitStack

import concourse.mybir as mybir

G, D, M, N = 4, 128, 128, 512
FLOPS = 4 * 2 * G * D * M * N

F32 = mybir.dt.float32
BF16 = mybir.dt.bfloat16
I32 = mybir.dt.int32
U32 = mybir.dt.uint32
U8 = mybir.dt.uint8
FP8X4 = mybir.dt.float8_e4m3fn_x4
ACT = mybir.ActivationFunctionType
ALU = mybir.AluOpType

P = 128
PACK = 4
ROWS = 32
W = 128
CHUNKS = N // W
WINDOW = 4
SLOTS = 3 * CHUNKS + 3
EPS = 1e-4
PAIRS = [(0, 2), (1, 3)]
SPANS = [(0, 1), (1, 3), (3, 4)]


def tile_rows_pl_cplx_mag_kernel(tc, xr, xi, wr, wi, out_0, out_1, out_2):
    nc = tc.nc

    def by_feature(t):
        return t.rearrange("g (p j) n -> (g p) j n", j=PACK)

    def read_order(raw):
        return raw.rearrange("p j (c i) -> p c j i", i=4)

    def write_order(packed):
        return packed.rearrange("p (c i) j -> p c j i", i=4)

    def quantize(codes, scales, packed):
        nc.vector.quantize_mx(out=codes.bitcast(FP8X4), scales=scales, in_=packed.rearrange("p n j -> p (n j)"))

    def columns(first, last):
        return slice(first * W, last * W)

    y_hbm = out_0.rearrange("(p u) n -> p u n", u=PACK)
    words_hbm = out_1[0].rearrange("p n u -> p (n u)").bitcast(I32)
    scales_hbm = out_2[0].bitcast(I32)

    with ExitStack() as ctx:
        sb = ctx.enter_context(tc.tile_pool(name="sb", bufs=1))
        ps = ctx.enter_context(tc.psum_pool(name="ps", bufs=1))
        ctx.enter_context(tc.manual_schedule())

        def tile(name, shape, dtype):
            return sb.tile(shape, dtype, name=name, align_bytes=64)

        def per_chunk(name, shape, dtype):
            return [tile("%s%d" % (name, c), shape, dtype) for c in range(CHUNKS)]

        wr_raw = tile("wr_raw", [P, PACK, M], F32)
        wi_raw = tile("wi_raw", [P, PACK, M], F32)
        w_pos = tile("w_pos", [P, 2 * M, PACK], BF16)
        w_neg = tile("w_neg", [P, M, PACK], BF16)
        w_codes = tile("w_codes", [P, 3 * M], U32)
        w_scales = tile("w_scales", [P, 3 * M], U8)
        one = tile("one", [P, 1], F32)
        eps = tile("eps", [P, 1], F32)

        xr_raw = [tile("xr_raw%d" % h, [P, PACK, 2 * W], F32) for h in range(2)]
        evicted = tile("evicted", [P, 2 * W], F32)
        y_last = tile("y_last", [P, G, W], F32)
        xi_raw = per_chunk("xi_raw", [P, PACK, W], F32)
        xr_packed = per_chunk("xr_packed", [P, W, PACK], BF16)
        xi_packed = per_chunk("xi_packed", [P, W, PACK], BF16)
        x_codes = tile("x_codes", [P, SLOTS * W], U32)
        x_scales = tile("x_scales", [P, SLOTS * W], U8)

        banks = [[ps.tile([P, WINDOW * W], F32, name="bank%d_%d" % (b, g)) for g in range(G)] for b in range(2)]
        squares = per_chunk("squares", [P, G, 2, W], F32)
        span_of = {c: s for s, (a, b) in enumerate(SPANS) for c in range(a, b)}
        sums = [tile("sums%d" % s, [P, G, (b - a) * W], F32) for s, (a, b) in enumerate(SPANS)]
        sums_rows = [tile("sums_rows%d" % s, [P, PACK, (b - a) * W], F32) for s, (a, b) in enumerate(SPANS)]
        y = [tile("y%d" % s, [P, PACK, (b - a) * W], F32) for s, (a, b) in enumerate(SPANS[:-1])]
        y_packed = per_chunk("y_packed", [P, W, PACK], BF16)
        y_codes = tile("y_codes", [P, N], U32)
        y_scales = tile("y_scales", [P, N], U8)

        def within(c):
            first = c - SPANS[span_of[c]][0]
            return columns(first, first + 1)

        def pack(packed, raw):
            nc.vector.tensor_copy(out=write_order(packed), in_=read_order(raw))

        def pack_on_scalar(packed, raw):
            nc.scalar.copy(out=write_order(packed), in_=read_order(raw))

        def product(c, step):
            w_cols = slice((1, 0, 2)[step] * M, ((1, 0, 2)[step] + 1) * M)
            x_cols = columns(3 * c + step, 3 * c + step + WINDOW)
            for g in (0, 2, 1, 3):
                rows = slice(ROWS * g, ROWS * (g + 1))
                nc.tensor.matmul_mx(
                    out=banks[c % 2][g][:],
                    lhsT=w_codes[rows, w_cols].bitcast(FP8X4),
                    lhsT_scale=w_scales[rows, w_cols],
                    rhs=x_codes[rows, x_cols].bitcast(FP8X4),
                    rhs_scale=x_scales[rows, x_cols],
                    start=step == 0,
                    stop=step == 2,
                )

        def quantize_xr(c):
            cols = columns(3 * c + 3, 3 * c + 4)
            quantize(x_codes[:, cols], x_scales[:, cols], xr_packed[c][:])

        def quantize_xi(c):
            cols = columns(3 * c + 4, 3 * c + 5)
            quantize(x_codes[:, cols], x_scales[:, cols], xi_packed[c][:])
            product(c, 1)
            product(c, 2)

        def regroup(s, g, eng):
            eng.dma_start(out=sums_rows[s][ROWS * g : ROWS * (g + 1), :, :], in_=sums[s][:, g, :])

        def square(c, groups):
            for g in groups:
                nc.scalar.activation(
                    out=squares[c][:, g, :, :].rearrange("p r n -> p (r n)"),
                    in_=banks[c % 2][g][:, columns(2, 4)],
                    func=ACT.Square,
                )

        def add(c, pair):
            groups = slice(pair[0], pair[-1] + 1, 2)
            nc.vector.tensor_tensor(
                out=sums[span_of[c]][:, groups, within(c)],
                in0=squares[c][:, groups, 0, :],
                in1=squares[c][:, groups, 1, :],
                op=ALU.add,
            )

        nc.sync.dma_start(out=wr_raw[:], in_=by_feature(wr))
        nc.sync.dma_start(out=wi_raw[:], in_=by_feature(wi))
        for c in range(CHUNKS):
            if c % 2 == 0:
                nc.sync.dma_start(out=xr_raw[c // 2][:], in_=by_feature(xr)[:, :, columns(c, c + 2)])
            nc.sync.dma_start(out=xi_raw[c][:], in_=by_feature(xi)[:, :, columns(c, c + 1)])

        nc.vector.memset(one[:], 1.0)
        nc.scalar.activation(out=eps[:], in_=one[:], func=ACT.Sqrt, scale=EPS * EPS)
        nc.vector.memset(x_codes[:], 0)
        nc.vector.memset(x_scales[:].bitcast(U32), 0)

        pack(w_pos[:, 0:M, :], wr_raw[:])
        pack(w_pos[:, M : 2 * M, :], wi_raw[:])
        nc.scalar.activation(out=write_order(w_neg[:]), in_=read_order(wi_raw[:]), func=ACT.Copy, scale=-1.0)
        quantize(w_codes[:, 0 : 2 * M], w_scales[:, 0 : 2 * M], w_pos[:])
        quantize(w_codes[:, 2 * M : 3 * M], w_scales[:, 2 * M : 3 * M], w_neg[:])
        pack(xr_packed[0][:], xr_raw[0][:, :, columns(0, 1)])
        pack_on_scalar(xr_packed[1][:], xr_raw[0][:, :, columns(1, 2)])
        quantize_xr(0)
        last = CHUNKS - 1
        product(0, 0)
        pack(xi_packed[0][:], xi_raw[0][:])
        quantize_xr(1)
        quantize_xi(0)
        square(0, (0, 2, 1, 3))
        product(1, 0)
        pack(xi_packed[1][:], xi_raw[1][:])
        quantize_xi(1)
        square(1, (0, 2, 1, 3))
        pack(xr_packed[2][:], xr_raw[1][:, :, columns(0, 1)])
        pack(xr_packed[3][:], xr_raw[1][:, :, columns(1, 2)])
        quantize_xr(2)
        product(2, 0)
        pack(xi_packed[2][:], xi_raw[2][:])
        quantize_xr(3)
        quantize_xi(2)
        product(last, 0)
        add(0, PAIRS[0])
        pack(xi_packed[last][:], xi_raw[last][:])
        add(0, PAIRS[1])
        quantize_xi(last)
        for g in (0, 2, 1, 3):
            regroup(0, g, nc.sync)
        for pair in PAIRS:
            add(1, pair)

        square(2, PAIRS[0])
        add(2, PAIRS[0])
        regroup(1, 0, nc.sync)
        square(2, PAIRS[1])
        regroup(1, 2, nc.scalar)
        add(2, PAIRS[1])
        regroup(1, 1, nc.sync)
        sums_of_3 = banks[last % 2][3][:, columns(2, 4)]
        nc.vector.tensor_copy(out=evicted[:], in_=sums_of_3)
        nc.vector.tensor_tensor(
            out=squares[last][:, 3, :, :].rearrange("p r n -> p (r n)"), in0=sums_of_3, in1=evicted[:], op=ALU.mult
        )
        add(last, (3,))
        regroup(2, 3, nc.sync)
        square(last, PAIRS[0])
        regroup(1, 3, nc.scalar)
        add(last, PAIRS[0])
        regroup(2, 0, nc.sync)
        square(last, (1,))
        regroup(2, 2, nc.scalar)
        add(last, (1,))
        regroup(2, 1, nc.sync)

        def root(out, in_):
            nc.scalar.activation(out=out, in_=in_, func=ACT.Sqrt, bias=eps[:])

        def quantize_y(c):
            cols = columns(c, c + 1)
            quantize(y_codes[:, cols], y_scales[:, cols], y_packed[c][:])

        for c in range(last):
            s = span_of[c]
            root(y[s][:, :, within(c)], sums_rows[s][:, :, within(c)])
            pack(y_packed[c][:], y[s][:, :, within(c)])
            if c == SPANS[s][1] - 1:
                nc.sync.dma_start(out=y_hbm[:, :, columns(*SPANS[s])], in_=y[s][:])
            if c == 0:
                root(y_last[:], sums[2][:])
                nc.sync.dma_start(out=out_0.rearrange("(g m) n -> m g n", g=G)[:, :, columns(last, CHUNKS)], in_=y_last[:])
            if c > 0:
                quantize_y(c - 1)
        quantize_y(last - 1)
        nc.sync.dma_start(out=words_hbm[:, columns(0, last)], in_=y_codes[:, columns(0, last)].bitcast(I32))

        root(write_order(y_packed[last][:]), read_order(sums_rows[2][:]))
        quantize_y(last)
        nc.sync.dma_start(out=words_hbm[:, columns(last, CHUNKS)], in_=y_codes[:, columns(last, CHUNKS)].bitcast(I32))
        for q in range(4):
            eng = nc.scalar if q % 2 == 0 else nc.sync
            eng.dma_start(out=scales_hbm[4 * q : 4 * q + 4, :], in_=y_scales[ROWS * q : ROWS * q + 4, :].bitcast(I32))
